import numpy as np
import ml_dtypes


def mxq(x, axis, fmt="e4m3"):
    dtype, down = {"e4m3": (ml_dtypes.float8_e4m3fn, 7), "e5m2": (ml_dtypes.float8_e5m2, 14)}[fmt]
    v = np.moveaxis(np.asarray(x, np.float32).astype(ml_dtypes.bfloat16).astype(np.float64), axis, -1)
    blocks = v.reshape(v.shape[:-1] + (-1, 32))
    amax = np.abs(blocks).max(-1, keepdims=True)
    byte = np.maximum(np.where(amax > 0, np.frexp(amax)[1] - 1 + 127, 0) - down, 1)
    scale = np.exp2(byte - 127.0)
    codes = (blocks / scale).astype(np.float32).astype(dtype).astype(np.float64)
    return np.moveaxis((codes * scale).reshape(v.shape), -1, axis)


WIDE = False


def mx_kscale(k):
    if not WIDE:
        return np.ones(k)
    levels = np.array([10, -10, 5, -5, 0])
    if k % 512:
        return np.exp2(np.random.permutation(np.resize(levels, k // 32))).repeat(32)
    a = np.empty((k // 512, 16))
    for p in range(k // 512):
        a[p, :8] = np.random.permutation(np.resize(levels, 8))
        for g in range(8):
            far = levels[np.abs(levels - a[p, g]) >= 10]
            a[p, g + 8] = far[np.random.randint(len(far))]
    return np.exp2(a.ravel()).repeat(32)


def f64(x):
    return np.asarray(x).astype(np.float64)


def striped(idx):
    return np.tile(idx.reshape(-1, 16).T, (8, 1)).astype(np.uint16)


def unstriped(offs):
    return offs[:16].T.reshape(-1).astype(np.int64)


E2M1 = np.array([0.0, 0.5, 1.0, 1.5, 2.0, 3.0, 4.0, 6.0, -0.0, -0.5, -1.0, -1.5, -2.0, -3.0, -4.0, -6.0])


def pack_weight(w, fmt):
    k, n = w.shape
    w = f64(np.asarray(w, np.float32).astype(ml_dtypes.bfloat16)).reshape(k // 32, 32, n)
    amax = np.abs(w).max(1)
    if fmt == "e4m3":
        byte = np.frexp(amax)[1] - 1 + 127 - 7
    else:
        mant, ex = np.frexp(amax / 6.0)
        byte = np.where(mant > 0.5, ex, ex - 1) + 127
    byte = np.clip(np.where(amax > 0, byte, 1), 1, 254)
    scaled = (w * np.exp2(127.0 - byte)[:, None, :]).reshape(k, n).astype(np.float32)
    by_word = np.ascontiguousarray(scaled.reshape(k // 512, 128, 4, n).transpose(0, 1, 3, 2))
    if fmt == "e4m3":
        words = by_word.astype(ml_dtypes.float8_e4m3fn).view(np.uint8)
    else:
        c = by_word.astype(ml_dtypes.float4_e2m1fn).view(np.uint8) & 0xF
        words = (c[..., 0::2] | (c[..., 1::2] << 4)).reshape(k // 512, 128, 2 * n)
    return np.ascontiguousarray(words), np.ascontiguousarray(byte.astype(np.uint8).reshape(k // 512, 16, n))


def unpack_weight(words, scales, fmt):
    g, _, n = scales.shape
    words = np.ascontiguousarray(words).reshape(g, 128, n, -1)
    if fmt == "e4m3":
        vals = words.view(ml_dtypes.float8_e4m3fn).astype(np.float64)
    else:
        nib = np.empty((g, 128, n, 4), np.uint8)
        nib[..., 0::2] = words & 0xF
        nib[..., 1::2] = words >> 4
        vals = E2M1[nib]
    vals = vals * np.repeat(np.exp2(scales.astype(np.float64) - 127.0), 8, axis=1)[..., None]
    return vals.transpose(0, 1, 3, 2).reshape(g * 512, n)


def gelu(v):
    return 0.5 * v * (1.0 + np.tanh(np.sqrt(2.0 / np.pi) * (v + 0.044715 * v**3)))


K, T, S, K2, H, N = 1024, 2048, 512, 512, 1024, 640


def setup_inputs():
    n = np.random.standard_normal
    s = mx_kscale(K)[:, None]
    s2 = mx_kscale(K2)[:, None]
    u = mx_kscale(H)[:, None]
    d = {}
    d["tab_words"], d["tab_scales"] = pack_weight(n((K, T)) * s, "e4m3")
    d["offs"] = striped(np.random.permutation(T)[:S])
    d["xs_words"], d["xs_scales"] = pack_weight(n((K2, S)) * s2, "e4m3")
    d["wa"] = (1.3 * n((K, H)) / s / K**0.5).astype(np.float32)
    d["ba"] = (0.6 * n(H)).astype(np.float32)
    d["wb_words"], d["wb_scales"] = pack_weight(1.3 * n((K, H)) / s * u.T / K**0.5, "e2m1")
    d["wd"] = (0.8 * n((K, H)) / s * u.T / K**0.5).astype(np.float32)
    d["wx"] = (0.9 * n((K2, H)) / s2 * u.T / K2**0.5).astype(np.float32)
    d["wo_words"], d["wo_scales"] = pack_weight(n((H, N)) / u / H**0.5, "e2m1")
    return d


def reference(tab_words, tab_scales, offs, xs_words, xs_scales, wa, ba, wb_words, wb_scales, wd, wx, wo_words, wo_scales):
    v = unpack_weight(tab_words, tab_scales, "e4m3")[:, unstriped(offs)]
    xs = unpack_weight(xs_words, xs_scales, "e4m3")
    wb = unpack_weight(wb_words, wb_scales, "e2m1")
    wo = unpack_weight(wo_words, wo_scales, "e2m1")
    a = (mxq(f64(wa), 0, "e4m3").T @ v) + f64(ba)[:, None]
    b = wb.T @ v
    low = mxq(f64(wd), 0, "e4m3").T @ v
    e = mxq(f64(wx), 0, "e4m3").T @ xs
    h = np.tanh(a) * b - low + e
    out = wo.T @ mxq(h, 0, "e4m3")
    return out

@@ -1,0 +1,305 @@
+from contextlib import ExitStack
+
+import concourse.mybir as mybir
+
+K, T, S, K2, H, N = 1024, 2048, 512, 512, 1024, 640
+FLOPS = 2 * S * (3 * K * H + K2 * H + H * N)
+
+F32 = mybir.dt.float32
+BF16 = mybir.dt.bfloat16
+I32 = mybir.dt.int32
+U32 = mybir.dt.uint32
+U16 = mybir.dt.uint16
+U8 = mybir.dt.uint8
+FP8X4 = mybir.dt.float8_e4m3fn_x4
+FP4X4 = mybir.dt.float4_e2m1fn_x4
+ACT = mybir.ActivationFunctionType
+ALU = mybir.AluOpType
+
+P = 128
+PACK = 4
+PASS = P * PACK
+CH = 128
+NCH = S // CH
+NT = N // P
+SCALAR_M = 96
+SCALAR_M_LAST = 24
+SHARE = {"wa00":128,"wa10":40,"wa01":0,"wa11":24,"wd00":0,"wd10":128,"wx0":96,"wd01":128,"wd11":112,"wx1":24}
+
+
+def tile_list_larval_feeding_scores_kernel(
+    tc, tab_words, tab_scales, offs, xs_words, xs_scales, wa, ba, wb_words, wb_scales, wd, wx, wo_words, wo_scales, out
+):
+    nc = tc.nc
+    with ExitStack() as ctx:
+        keep = ctx.enter_context(tc.tile_pool(name="keep", bufs=1))
+        ring = ctx.enter_context(tc.tile_pool(name="ring", bufs=4))
+        psum = ctx.enter_context(tc.psum_pool(name="psum", bufs=1))
+
+        def sb(name, shape, dtype):
+            return keep.tile(shape, dtype, name=name, align_bytes=64)
+
+        offsets = sb("offsets", [P, S // 16], U16)
+        xbank = [psum.tile([P, PASS], F32, name=f"xbank{i}") for i in range(4)]
+        ebank = [psum.tile([P, PASS], F32, name=f"ebank{i}") for i in range(4)]
+
+        tab_plane = sb("tab_plane", [P, 2, T], U8)
+        wb_plane_raw = sb("wb_plane_raw", [P, 2, H], U8)
+        xs_plane = sb("xs_plane", [P, S], U8)
+        wo_plane = sb("wo_plane", [P, 2, N], U8)
+        for plane in (tab_plane, wb_plane_raw, xs_plane, wo_plane):
+            nc.vector.memset(plane[:].bitcast(I32), 0)
+
+        def load_weight(name, w, g, b, halves=1):
+            raw = sb(name + "_raw", [P, PACK, PASS], F32)
+            rows = w[g * PASS : (g + 1) * PASS, b * PASS : (b + 1) * PASS].rearrange("(p j) c -> p j c", j=PACK)
+            if halves == PACK:
+                for j in range(PACK):
+                    nc.sync.dma_start(out=raw[:, j, :], in_=rows[:, j, :])
+                return raw
+            step = PASS // halves
+            for c0 in range(0, PASS, step):
+                nc.sync.dma_start(out=raw[:, :, c0 : c0 + step], in_=rows[:, :, c0 : c0 + step])
+            return raw
+
+        def quantise_weight(name, raw, sign, halves=1):
+            scalar_m = SHARE[name]
+            grouped = ring.tile([P, PACK, P, PACK], BF16, name="grouped", align_bytes=64)
+            codes = sb(name + "_codes", [P, PASS], U32)
+            plane = sb(name + "_plane", [P, PASS], U8)
+            src = raw[:].rearrange("p j (m t) -> p m j t", t=PACK)
+            dst = grouped[:].rearrange("p t m j -> p m j t")
+            step = P // halves
+            for m0 in range(0, P, step):
+                mid, m1 = m0 + scalar_m, m0 + step
+                if mid > m0:
+                    nc.scalar.activation(out=dst[:, m0:mid], in_=src[:, m0:mid], func=ACT.Copy, scale=sign)
+                if m1 > mid:
+                    nc.vector.tensor_scalar(out=dst[:, mid:m1], in0=src[:, mid:m1], scalar1=sign, scalar2=None, op0=ALU.mult)
+            nc.vector.quantize_mx(
+                out=codes[:].bitcast(FP8X4), scales=plane[:], in_=grouped[:].rearrange("p t m j -> p (t m j)")
+            )
+            return codes, plane
+
+        wb_raw = sb("wb_raw", [P, 2, H], U16)
+        bias = sb("bias", [P, 2, PACK], F32)
+        tab = [sb(f"tab{g}", [P, T], U32) for g in range(2)]
+        xs_codes = sb("xs_codes", [P, S], U32)
+        wo_codes = sb("wo_codes", [P, 2, N], U16)
+        wa_raw, wd_raw, wx_raw = {}, {}, {}
+
+        def load_plane(plane, scales, eng=nc.sync):
+            for q in range(4):
+                eng.dma_start(
+                    out=plane[32 * q : 32 * q + 4].bitcast(I32),
+                    in_=scales[:, 4 * q : 4 * q + 4, :].rearrange("g r n -> r g n").bitcast(I32),
+                )
+
+        def load_tab(g, parts):
+            words = tab_words[g].rearrange("p n t -> p (n t)").bitcast(I32)
+            for c0 in range(0, T, T // parts):
+                nc.sync.dma_start(out=tab[g][:, c0 : c0 + T // parts].bitcast(I32), in_=words[:, c0 : c0 + T // parts])
+
+        nc.sync.dma_start(offsets[:], offs)
+        nc.sync.dma_start(out=bias[:], in_=ba.rearrange("(b p t) -> p b t", b=2, t=PACK))
+        for g in range(2):
+            nc.sync.dma_start(out=wb_raw[:, g, :].bitcast(I32), in_=wb_words[g].bitcast(I32))
+        load_tab(0, 2)
+        load_plane(tab_plane, tab_scales)
+        wa_raw[0, 0] = load_weight("wa00", wa, 0, 0, halves=1)
+        load_plane(wb_plane_raw, wb_scales)
+        load_tab(1, 1)
+        wa_raw[1, 0] = load_weight("wa10", wa, 1, 0, halves=1)
+        wa_raw[0, 1] = load_weight("wa01", wa, 0, 1, halves=1)
+        wa_raw[1, 1] = load_weight("wa11", wa, 1, 1, halves=1)
+        wd_raw[0, 0] = load_weight("wd00", wd, 0, 0, halves=1)
+        nc.sync.dma_start(out=xs_codes[:].bitcast(I32), in_=xs_words[0].rearrange("p n t -> p (n t)").bitcast(I32))
+        for q in range(4):
+            nc.sync.dma_start(
+                out=xs_plane[32 * q + 4 : 32 * q + 8, :].bitcast(I32), in_=xs_scales[0, 4 * q : 4 * q + 4, :].bitcast(I32)
+            )
+        wd_raw[1, 0] = load_weight("wd10", wd, 1, 0, halves=1)
+        wx_raw[0] = load_weight("wx0", wx, 0, 0, halves=1)
+        wd_raw[0, 1] = load_weight("wd01", wd, 0, 1, halves=1)
+        load_plane(wo_plane, wo_scales)
+        nc.sync.dma_start(out=wo_codes[:].bitcast(I32), in_=wo_words.rearrange("g p c -> p g c").bitcast(I32))
+        wd_raw[1, 1] = load_weight("wd11", wd, 1, 1, halves=1)
+        wx_raw[1] = load_weight("wx1", wx, 0, 1, halves=2)
+
+        wb_codes = sb("wb_codes", [P, 2, 2, PASS], U16)
+        for b in range(2):
+            for g in range(2):
+                nc.scalar.copy(
+                    out=wb_codes[:, g, b, :].rearrange("p (t u i) -> p u t i", t=PACK, i=8),
+                    in_=wb_raw[:, g, b * PASS : (b + 1) * PASS].rearrange("p (u i t) -> p u t i", t=PACK, i=8),
+                )
+
+        v_plane = [sb(f"v_plane{g}", [P, S], U8) for g in range(2)]
+        v_codes = [sb(f"v_codes{g}", [P, S], U32) for g in range(2)]
+        wb_plane = sb("wb_plane", [P, 2, 2, PASS], U8)
+
+        def gather_words(g):
+            nc.vector.tensor_copy(v_codes[g][:], tab[g][:].indirect(offsets[:]))
+
+        def gather_scales(g):
+            nc.vector.tensor_copy(v_plane[g][:], tab_plane[:, g, :].indirect(offsets[:]))
+
+        def deal_wb_scales(b):
+            nc.vector.tensor_copy(
+                out=wb_plane[:, :, b, :].rearrange("p g (t u i) -> p g u t i", t=PACK, i=16),
+                in_=wb_plane_raw[:, :, b * PASS : (b + 1) * PASS].rearrange("p g (u i t) -> p g u t i", t=PACK, i=16),
+            )
+
+        def v_scales(g, cols):
+            return v_plane[g][:, cols]
+
+        def product_b(b, g, banks):
+            for c in range(NCH):
+                cols = slice(c * CH, (c + 1) * CH)
+                for t in range(PACK):
+                    tc_ = slice(t * P, (t + 1) * P)
+                    nc.tensor.matmul_mx(
+                        out=banks[c][:, tc_],
+                        lhsT=wb_codes[:, g, b, tc_].bitcast(FP4X4),
+                        lhsT_scale=wb_plane[:, g, b, tc_],
+                        rhs=v_codes[g][:, cols].bitcast(FP8X4),
+                        rhs_scale=v_scales(g, cols),
+                        start=(g == 0 and t == 0),
+                        stop=(g == 1 and t == PACK - 1),
+                    )
+
+        def product_a(b, g):
+            codes, plane = wq[f"wa{g}{b}"]
+            for t in range(PACK):
+                tc_ = slice(t * P, (t + 1) * P)
+                nc.tensor.matmul_mx(
+                    out=xbank[t][:],
+                    lhsT=codes[:, tc_].bitcast(FP8X4),
+                    lhsT_scale=plane[:, tc_],
+                    rhs=v_codes[g][:].bitcast(FP8X4),
+                    rhs_scale=v_scales(g, slice(0, S)),
+                    start=(g == 0),
+                    stop=(g == 1),
+                )
+
+        def squash(b):
+            tanh_a = sb(f"tanh{b}", [P, PACK, S], F32)
+            for t in range(PACK):
+                nc.scalar.activation(out=tanh_a[:, t, :], in_=xbank[t][:], func=ACT.Tanh, bias=bias[:, b, t : t + 1])
+            return tanh_a
+
+        def gate(b, tanh_a, banks):
+            prods = []
+            for c in range(NCH):
+                prod = sb(f"prod{b}{c}", [P, CH, PACK], F32)
+                nc.vector.tensor_tensor(
+                    out=prod[:],
+                    in0=banks[c][:].rearrange("p (t j) -> p j t", t=PACK),
+                    in1=tanh_a[:, :, c * CH : (c + 1) * CH].rearrange("p t j -> p j t"),
+                    op=ALU.mult,
+                )
+                prods.append(prod)
+            return prods
+
+        def product_d(banks, weights, moving, moving_plane, first, last):
+            codes, plane = weights
+            for c in range(NCH):
+                cols = slice(c * CH, (c + 1) * CH)
+                for t in range(PACK):
+                    tc_ = slice(t * P, (t + 1) * P)
+                    nc.tensor.matmul_mx(
+                        out=banks[c][:, tc_],
+                        lhsT=codes[:, tc_].bitcast(FP8X4),
+                        lhsT_scale=plane[:, tc_],
+                        rhs=moving[:, cols].bitcast(FP8X4),
+                        rhs_scale=moving_plane(cols),
+                        start=(first and t == 0),
+                        stop=(last and t == PACK - 1),
+                    )
+
+        def features(b, c, prod, bank):
+            h = sb(f"h{b}{c}", [P, CH, PACK], BF16)
+            nc.vector.tensor_tensor(
+                out=h[:], in0=prod[:], in1=bank[:].rearrange("p (t j) -> p j t", t=PACK), op=ALU.subtract
+            )
+            return h
+
+        def quantise_h(b, c, h):
+            codes = sb(f"h{b}{c}_codes", [P, CH], U32)
+            plane = sb(f"h{b}{c}_plane", [P, CH], U8)
+            nc.vector.quantize_mx(out=codes[:].bitcast(FP8X4), scales=plane[:], in_=h[:].rearrange("p j t -> p (j t)"))
+            return codes, plane
+
+        def score_pass(dst, g, nt, hq, start, stop):
+            rows = slice(nt * P, (nt + 1) * P)
+            nc.tensor.matmul_mx(
+                out=dst,
+                lhsT=wo_codes[:, g, rows].bitcast(FP4X4),
+                lhsT_scale=wo_plane[:, g, rows],
+                rhs=hq[0][:].bitcast(FP8X4),
+                rhs_scale=hq[1][:],
+                start=start,
+                stop=stop,
+            )
+
+        def xs_scales_at(cols):
+            return xs_plane[4:, cols]
+
+        wq, tanh_a, prod = {}, {}, {}
+        gather_words(0)
+        gather_scales(0)
+        gather_scales(1)
+        deal_wb_scales(0)
+        deal_wb_scales(1)
+        gather_words(1)
+        wq["wa00"] = quantise_weight("wa00", wa_raw[0, 0], 1.0)
+        wq["wa10"] = quantise_weight("wa10", wa_raw[1, 0], 1.0)
+        product_a(0, 0)
+        product_a(0, 1)
+        product_b(0, 0, ebank)
+        product_b(0, 1, ebank)
+        tanh_a[0] = squash(0)
+        wq["wa01"] = quantise_weight("wa01", wa_raw[0, 1], 1.0)
+        product_a(1, 0)
+        wq["wa11"] = quantise_weight("wa11", wa_raw[1, 1], 1.0)
+        product_a(1, 1)
+        tanh_a[1] = squash(1)
+        prod[0] = gate(0, tanh_a[0], ebank)
+        product_b(1, 0, ebank)
+        product_b(1, 1, ebank)
+        wq["wd00"] = quantise_weight("wd00", wd_raw[0, 0], 1.0)
+        wq["wd10"] = quantise_weight("wd10", wd_raw[1, 0], 1.0)
+        wq["wx0"] = quantise_weight("wx0", wx_raw[0], -1.0)
+        prod[1] = gate(1, tanh_a[1], ebank)
+        product_d(xbank, wq["wd00"], v_codes[0], lambda cols: v_scales(0, cols), True, False)
+        product_d(xbank, wq["wd10"], v_codes[1], lambda cols: v_scales(1, cols), False, False)
+        product_d(xbank, wq["wx0"], xs_codes, xs_scales_at, False, True)
+        wq["wd01"] = quantise_weight("wd01", wd_raw[0, 1], 1.0)
+        product_d(ebank, wq["wd01"], v_codes[0], lambda cols: v_scales(0, cols), True, False)
+        wq["wd11"] = quantise_weight("wd11", wd_raw[1, 1], 1.0)
+        product_d(ebank, wq["wd11"], v_codes[1], lambda cols: v_scales(1, cols), False, False)
+        h0 = [features(0, c, prod[0][c], xbank[c]) for c in range(NCH)]
+        hq0 = [quantise_h(0, c, h0[c]) for c in range(NCH)]
+        for c in range(NCH):
+            for nt in range(NT - 1):
+                score_pass(xbank[c][:, nt * CH : (nt + 1) * CH], 0, nt, hq0[c], nt == 0, False)
+        wq["wx1"] = quantise_weight("wx1", wx_raw[1], -1.0, halves=2)
+        product_d(ebank, wq["wx1"], xs_codes, xs_scales_at, False, True)
+
+        out_rows = out.rearrange("(nt p) j -> p nt j", p=P)
+        h1 = [features(1, 0, prod[1][0], ebank[0])]
+        for c in range(NCH):
+            if c + 1 < NCH:
+                h1.append(features(1, c + 1, prod[1][c + 1], ebank[c + 1]))
+            hq1 = quantise_h(1, c, h1[c])
+            score_pass(ebank[c][:, 0:CH], 0, NT - 1, hq0[c], True, False)
+            for nt in range(NT - 1):
+                score_pass(xbank[c][:, nt * CH : (nt + 1) * CH], 1, nt, hq1, False, nt == NT - 2)
+            score_pass(ebank[c][:, 0:CH], 1, NT - 1, hq1, False, True)
+            scores = sb(f"scores{c}", [P, NT, CH], F32)
+            nc.scalar.copy(out=scores[:, 0 : NT - 1, :].rearrange("p n j -> p (n j)"), in_=xbank[c][:])
+            if c + 1 < NCH:
+                nc.scalar.copy(out=scores[:, NT - 1, :], in_=ebank[c][:, 0:CH])
+            else:
+                nc.vector.tensor_copy(out=scores[:, NT - 1, :], in_=ebank[c][:, 0:CH])
+            nc.sync.dma_start(out=out_rows[:, :, c * CH : (c + 1) * CH], in_=scores[:])

@@ -24,7 +24,7 @@ NCH = S // CH
 NT = N // P
 SCALAR_M = 96
 SCALAR_M_LAST = 24
-SHARE = {"wa00":128,"wa10":40,"wa01":0,"wa11":24,"wd00":0,"wd10":128,"wx0":96,"wd01":128,"wd11":112,"wx1":24}
+SHARE = {"wa00":128,"wa10":40,"wa01":0,"wa11":24,"wd00":48,"wd10":128,"wx0":32,"wd01":128,"wd11":128,"wx1":24}
 
 
 def tile_list_larval_feeding_scores_kernel(
@@ -67,15 +67,18 @@ def tile_list_larval_feeding_scores_kernel(
             grouped = ring.tile([P, PACK, P, PACK], BF16, name="grouped", align_bytes=64)
             codes = sb(name + "_codes", [P, PASS], U32)
             plane = sb(name + "_plane", [P, PASS], U8)
-            src = raw[:].rearrange("p j (m t) -> p m j t", t=PACK)
-            dst = grouped[:].rearrange("p t m j -> p m j t")
+            src = raw[:].rearrange("p j (m u i) -> p u m j i", u=2, i=2)
+            dst = grouped[:].rearrange("p (u i) m j -> p u m j i", i=2)
             step = P // halves
             for m0 in range(0, P, step):
                 mid, m1 = m0 + scalar_m, m0 + step
-                if mid > m0:
-                    nc.scalar.activation(out=dst[:, m0:mid], in_=src[:, m0:mid], func=ACT.Copy, scale=sign)
-                if m1 > mid:
-                    nc.vector.tensor_scalar(out=dst[:, mid:m1], in0=src[:, mid:m1], scalar1=sign, scalar2=None, op0=ALU.mult)
+                for u in range(2):
+                    if mid > m0:
+                        nc.scalar.activation(out=dst[:, u, m0:mid], in_=src[:, u, m0:mid], func=ACT.Copy, scale=sign)
+                    if m1 > mid:
+                        nc.vector.tensor_scalar(
+                            out=dst[:, u, mid:m1], in0=src[:, u, mid:m1], scalar1=sign, scalar2=None, op0=ALU.mult
+                        )
             nc.vector.quantize_mx(
                 out=codes[:].bitcast(FP8X4), scales=plane[:], in_=grouped[:].rearrange("p t m j -> p (t m j)")
             )
@@ -89,10 +92,10 @@ def tile_list_larval_feeding_scores_kernel(
         wa_raw, wd_raw, wx_raw = {}, {}, {}
 
         def load_plane(plane, scales, eng=nc.sync):
-            for q in range(4):
+            for r in range(4):
                 eng.dma_start(
-                    out=plane[32 * q : 32 * q + 4].bitcast(I32),
-                    in_=scales[:, 4 * q : 4 * q + 4, :].rearrange("g r n -> r g n").bitcast(I32),
+                    out=plane[r:P:32].bitcast(I32),
+                    in_=scales[:, r:16:4, :].rearrange("g q n -> q g n").bitcast(I32),
                 )
 
         def load_tab(g, parts):
@@ -114,16 +117,16 @@ def tile_list_larval_feeding_scores_kernel(
         wa_raw[1, 1] = load_weight("wa11", wa, 1, 1, halves=1)
         wd_raw[0, 0] = load_weight("wd00", wd, 0, 0, halves=1)
         nc.sync.dma_start(out=xs_codes[:].bitcast(I32), in_=xs_words[0].rearrange("p n t -> p (n t)").bitcast(I32))
-        for q in range(4):
+        for r in range(4):
             nc.sync.dma_start(
-                out=xs_plane[32 * q + 4 : 32 * q + 8, :].bitcast(I32), in_=xs_scales[0, 4 * q : 4 * q + 4, :].bitcast(I32)
+                out=xs_plane[4 + r : P : 32, :].bitcast(I32), in_=xs_scales[0, r:16:4, :].bitcast(I32)
             )
         wd_raw[1, 0] = load_weight("wd10", wd, 1, 0, halves=1)
         wx_raw[0] = load_weight("wx0", wx, 0, 0, halves=1)
         wd_raw[0, 1] = load_weight("wd01", wd, 0, 1, halves=1)
+        wd_raw[1, 1] = load_weight("wd11", wd, 1, 1, halves=1)
         load_plane(wo_plane, wo_scales)
         nc.sync.dma_start(out=wo_codes[:].bitcast(I32), in_=wo_words.rearrange("g p c -> p g c").bitcast(I32))
-        wd_raw[1, 1] = load_weight("wd11", wd, 1, 1, halves=1)
         wx_raw[1] = load_weight("wx1", wx, 0, 1, halves=2)
 
         wb_codes = sb("wb_codes", [P, 2, 2, PASS], U16)
@@ -154,19 +157,17 @@ def tile_list_larval_feeding_scores_kernel(
             return v_plane[g][:, cols]
 
         def product_b(b, g, banks):
-            for c in range(NCH):
-                cols = slice(c * CH, (c + 1) * CH)
-                for t in range(PACK):
-                    tc_ = slice(t * P, (t + 1) * P)
-                    nc.tensor.matmul_mx(
-                        out=banks[c][:, tc_],
-                        lhsT=wb_codes[:, g, b, tc_].bitcast(FP4X4),
-                        lhsT_scale=wb_plane[:, g, b, tc_],
-                        rhs=v_codes[g][:, cols].bitcast(FP8X4),
-                        rhs_scale=v_scales(g, cols),
-                        start=(g == 0 and t == 0),
-                        stop=(g == 1 and t == PACK - 1),
-                    )
+            for t in range(PACK):
+                tc_ = slice(t * P, (t + 1) * P)
+                nc.tensor.matmul_mx(
+                    out=banks[t][:],
+                    lhsT=wb_codes[:, g, b, tc_].bitcast(FP4X4),
+                    lhsT_scale=wb_plane[:, g, b, tc_],
+                    rhs=v_codes[g][:].bitcast(FP8X4),
+                    rhs_scale=v_plane[g][:],
+                    start=(g == 0),
+                    stop=(g == 1),
+                )
 
         def product_a(b, g):
             codes, plane = wq[f"wa{g}{b}"]
@@ -189,21 +190,14 @@ def tile_list_larval_feeding_scores_kernel(
             return tanh_a
 
         def gate(b, tanh_a, banks):
-            prods = []
-            for c in range(NCH):
-                prod = sb(f"prod{b}{c}", [P, CH, PACK], F32)
-                nc.vector.tensor_tensor(
-                    out=prod[:],
-                    in0=banks[c][:].rearrange("p (t j) -> p j t", t=PACK),
-                    in1=tanh_a[:, :, c * CH : (c + 1) * CH].rearrange("p t j -> p j t"),
-                    op=ALU.mult,
-                )
-                prods.append(prod)
-            return prods
+            prod = sb(f"prod{b}", [P, PACK, S], F32)
+            for t in range(PACK):
+                nc.vector.tensor_tensor(out=prod[:, t, :], in0=banks[t][:], in1=tanh_a[:, t, :], op=ALU.mult)
+            return prod
 
-        def product_d(banks, weights, moving, moving_plane, first, last):
+        def product_d(banks, weights, moving, moving_plane, first, last, chunks=range(NCH)):
             codes, plane = weights
-            for c in range(NCH):
+            for c in chunks:
                 cols = slice(c * CH, (c + 1) * CH)
                 for t in range(PACK):
                     tc_ = slice(t * P, (t + 1) * P)
@@ -220,7 +214,10 @@ def tile_list_larval_feeding_scores_kernel(
         def features(b, c, prod, bank):
             h = sb(f"h{b}{c}", [P, CH, PACK], BF16)
             nc.vector.tensor_tensor(
-                out=h[:], in0=prod[:], in1=bank[:].rearrange("p (t j) -> p j t", t=PACK), op=ALU.subtract
+                out=h[:].rearrange("p (q i) t -> p q t i", i=2),
+                in0=prod[:, :, c * CH : (c + 1) * CH].rearrange("p t (q i) -> p q t i", i=2),
+                in1=bank[:].rearrange("p (t q i) -> p q t i", t=PACK, i=2),
+                op=ALU.subtract,
             )
             return h
 
@@ -272,25 +269,27 @@ def tile_list_larval_feeding_scores_kernel(
         wq["wx0"] = quantise_weight("wx0", wx_raw[0], -1.0)
         prod[1] = gate(1, tanh_a[1], ebank)
         product_d(xbank, wq["wd00"], v_codes[0], lambda cols: v_scales(0, cols), True, False)
-        product_d(xbank, wq["wd10"], v_codes[1], lambda cols: v_scales(1, cols), False, False)
-        product_d(xbank, wq["wx0"], xs_codes, xs_scales_at, False, True)
+        for c in range(NCH):
+            product_d(xbank, wq["wd10"], v_codes[1], lambda cols: v_scales(1, cols), False, False, [c])
+            product_d(xbank, wq["wx0"], xs_codes, xs_scales_at, False, True, [c])
         wq["wd01"] = quantise_weight("wd01", wd_raw[0, 1], 1.0)
         product_d(ebank, wq["wd01"], v_codes[0], lambda cols: v_scales(0, cols), True, False)
         wq["wd11"] = quantise_weight("wd11", wd_raw[1, 1], 1.0)
-        product_d(ebank, wq["wd11"], v_codes[1], lambda cols: v_scales(1, cols), False, False)
-        h0 = [features(0, c, prod[0][c], xbank[c]) for c in range(NCH)]
+        wq["wx1"] = quantise_weight("wx1", wx_raw[1], -1.0, halves=2)
+        for c in range(NCH):
+            product_d(ebank, wq["wd11"], v_codes[1], lambda cols: v_scales(1, cols), False, False, [c])
+            product_d(ebank, wq["wx1"], xs_codes, xs_scales_at, False, True, [c])
+        h0 = [features(0, c, prod[0], xbank[c]) for c in range(NCH)]
         hq0 = [quantise_h(0, c, h0[c]) for c in range(NCH)]
         for c in range(NCH):
             for nt in range(NT - 1):
                 score_pass(xbank[c][:, nt * CH : (nt + 1) * CH], 0, nt, hq0[c], nt == 0, False)
-        wq["wx1"] = quantise_weight("wx1", wx_raw[1], -1.0, halves=2)
-        product_d(ebank, wq["wx1"], xs_codes, xs_scales_at, False, True)
 
         out_rows = out.rearrange("(nt p) j -> p nt j", p=P)
-        h1 = [features(1, 0, prod[1][0], ebank[0])]
+        h1 = [features(1, 0, prod[1], ebank[0])]
         for c in range(NCH):
             if c + 1 < NCH:
-                h1.append(features(1, c + 1, prod[1][c + 1], ebank[c + 1]))
+                h1.append(features(1, c + 1, prod[1], ebank[c + 1]))
             hq1 = quantise_h(1, c, h1[c])
             score_pass(ebank[c][:, 0:CH], 0, NT - 1, hq0[c], True, False)
             for nt in range(NT - 1):

@@ -24,7 +24,7 @@ NCH = S // CH
 NT = N // P
 SCALAR_M = 96
 SCALAR_M_LAST = 24
-SHARE = {"wa00":128,"wa10":40,"wa01":0,"wa11":24,"wd00":48,"wd10":128,"wx0":32,"wd01":128,"wd11":128,"wx1":24}
+SHARE = {"wa00":128,"wa10":64,"wa01":40,"wa11":40,"wd00":64,"wd10":96,"wx0":64,"wd01":128,"wd11":112,"wx1":24}
 
 
 def tile_list_larval_feeding_scores_kernel(
@@ -47,8 +47,11 @@ def tile_list_larval_feeding_scores_kernel(
         wb_plane_raw = sb("wb_plane_raw", [P, 2, H], U8)
         xs_plane = sb("xs_plane", [P, S], U8)
         wo_plane = sb("wo_plane", [P, 2, N], U8)
-        for plane in (tab_plane, wb_plane_raw, xs_plane, wo_plane):
-            nc.vector.memset(plane[:].bitcast(I32), 0)
+        nc.vector.memset(tab_plane[:, 0, :].bitcast(I32), 0)
+        nc.gpsimd.memset(tab_plane[:, 1, :].bitcast(I32), 0)
+        nc.vector.memset(wb_plane_raw[:].bitcast(I32), 0)
+        for plane in (xs_plane, wo_plane):
+            nc.gpsimd.memset(plane[:].bitcast(I32), 0)
 
         def load_weight(name, w, g, b, halves=1):
             raw = sb(name + "_raw", [P, PACK, PASS], F32)
@@ -105,12 +108,11 @@ def tile_list_larval_feeding_scores_kernel(
 
         nc.sync.dma_start(offsets[:], offs)
         nc.sync.dma_start(out=bias[:], in_=ba.rearrange("(b p t) -> p b t", b=2, t=PACK))
-        for g in range(2):
-            nc.sync.dma_start(out=wb_raw[:, g, :].bitcast(I32), in_=wb_words[g].bitcast(I32))
-        load_tab(0, 2)
+        nc.sync.dma_start(out=wb_raw[:].bitcast(I32), in_=wb_words.rearrange("g p c -> p g c").bitcast(I32))
         load_plane(tab_plane, tab_scales)
-        wa_raw[0, 0] = load_weight("wa00", wa, 0, 0, halves=1)
+        load_tab(0, 1)
         load_plane(wb_plane_raw, wb_scales)
+        wa_raw[0, 0] = load_weight("wa00", wa, 0, 0, halves=1)
         load_tab(1, 1)
         wa_raw[1, 0] = load_weight("wa10", wa, 1, 0, halves=1)
         wa_raw[0, 1] = load_weight("wa01", wa, 0, 1, halves=1)
@@ -124,9 +126,9 @@ def tile_list_larval_feeding_scores_kernel(
         wd_raw[1, 0] = load_weight("wd10", wd, 1, 0, halves=1)
         wx_raw[0] = load_weight("wx0", wx, 0, 0, halves=1)
         wd_raw[0, 1] = load_weight("wd01", wd, 0, 1, halves=1)
-        wd_raw[1, 1] = load_weight("wd11", wd, 1, 1, halves=1)
         load_plane(wo_plane, wo_scales)
         nc.sync.dma_start(out=wo_codes[:].bitcast(I32), in_=wo_words.rearrange("g p c -> p g c").bitcast(I32))
+        wd_raw[1, 1] = load_weight("wd11", wd, 1, 1, halves=1)
         wx_raw[1] = load_weight("wx1", wx, 0, 1, halves=2)
 
         wb_codes = sb("wb_codes", [P, 2, 2, PASS], U16)
@@ -243,13 +245,13 @@ def tile_list_larval_feeding_scores_kernel(
             return xs_plane[4:, cols]
 
         wq, tanh_a, prod = {}, {}, {}
-        gather_words(0)
         gather_scales(0)
         gather_scales(1)
+        gather_words(0)
         deal_wb_scales(0)
-        deal_wb_scales(1)
         gather_words(1)
         wq["wa00"] = quantise_weight("wa00", wa_raw[0, 0], 1.0)
+        deal_wb_scales(1)
         wq["wa10"] = quantise_weight("wa10", wa_raw[1, 0], 1.0)
         product_a(0, 0)
         product_a(0, 1)
@@ -275,15 +277,14 @@ def tile_list_larval_feeding_scores_kernel(
         wq["wd01"] = quantise_weight("wd01", wd_raw[0, 1], 1.0)
         product_d(ebank, wq["wd01"], v_codes[0], lambda cols: v_scales(0, cols), True, False)
         wq["wd11"] = quantise_weight("wd11", wd_raw[1, 1], 1.0)
-        wq["wx1"] = quantise_weight("wx1", wx_raw[1], -1.0, halves=2)
-        for c in range(NCH):
-            product_d(ebank, wq["wd11"], v_codes[1], lambda cols: v_scales(1, cols), False, False, [c])
-            product_d(ebank, wq["wx1"], xs_codes, xs_scales_at, False, True, [c])
+        product_d(ebank, wq["wd11"], v_codes[1], lambda cols: v_scales(1, cols), False, False)
         h0 = [features(0, c, prod[0], xbank[c]) for c in range(NCH)]
         hq0 = [quantise_h(0, c, h0[c]) for c in range(NCH)]
         for c in range(NCH):
             for nt in range(NT - 1):
                 score_pass(xbank[c][:, nt * CH : (nt + 1) * CH], 0, nt, hq0[c], nt == 0, False)
+        wq["wx1"] = quantise_weight("wx1", wx_raw[1], -1.0, halves=2)
+        product_d(ebank, wq["wx1"], xs_codes, xs_scales_at, False, True)
 
         out_rows = out.rearrange("(nt p) j -> p nt j", p=P)
         h1 = [features(1, 0, prod[1], ebank[0])]

@@ -24,7 +24,7 @@ NCH = S // CH
 NT = N // P
 SCALAR_M = 96
 SCALAR_M_LAST = 24
-SHARE = {"wa00":128,"wa10":64,"wa01":40,"wa11":40,"wd00":64,"wd10":96,"wx0":64,"wd01":128,"wd11":112,"wx1":24}
+SHARE = {"wa00":128,"wa10":64,"wa01":40,"wa11":40,"wd00":64,"wd10":32,"wx0":48,"wd01":80,"wd11":80,"wx1":24}
 
 
 def tile_list_larval_feeding_scores_kernel(
@@ -74,7 +74,8 @@ def tile_list_larval_feeding_scores_kernel(
             dst = grouped[:].rearrange("p (u i) m j -> p u m j i", i=2)
             step = P // halves
             for m0 in range(0, P, step):
-                mid, m1 = m0 + scalar_m, m0 + step
+                m1 = m0 + step
+                mid = m1 if m1 < P and halves > 1 else m0 + scalar_m
                 for u in range(2):
                     if mid > m0:
                         nc.scalar.activation(out=dst[:, u, m0:mid], in_=src[:, u, m0:mid], func=ACT.Copy, scale=sign)
@@ -82,16 +83,21 @@ def tile_list_larval_feeding_scores_kernel(
                         nc.vector.tensor_scalar(
                             out=dst[:, u, mid:m1], in0=src[:, u, mid:m1], scalar1=sign, scalar2=None, op0=ALU.mult
                         )
-            nc.vector.quantize_mx(
-                out=codes[:].bitcast(FP8X4), scales=plane[:], in_=grouped[:].rearrange("p t m j -> p (t m j)")
-            )
+            for u in range(halves):
+                ts_ = slice(u * PACK // halves, (u + 1) * PACK // halves)
+                cols = slice(ts_.start * P, ts_.stop * P)
+                nc.vector.quantize_mx(
+                    out=codes[:, cols].bitcast(FP8X4),
+                    scales=plane[:, cols],
+                    in_=grouped[:, ts_].rearrange("p t m j -> p (t m j)"),
+                )
             return codes, plane
 
         wb_raw = sb("wb_raw", [P, 2, H], U16)
         bias = sb("bias", [P, 2, PACK], F32)
         tab = [sb(f"tab{g}", [P, T], U32) for g in range(2)]
         xs_codes = sb("xs_codes", [P, S], U32)
-        wo_codes = sb("wo_codes", [P, 2, N], U16)
+        wo_codes = [sb(f"wo_codes{g}", [P, N], U16) for g in range(2)]
         wa_raw, wd_raw, wx_raw = {}, {}, {}
 
         def load_plane(plane, scales, eng=nc.sync):
@@ -112,6 +118,11 @@ def tile_list_larval_feeding_scores_kernel(
         load_plane(tab_plane, tab_scales)
         load_tab(0, 1)
         load_plane(wb_plane_raw, wb_scales)
+        for r in range(4):
+            nc.gpsimd.dma_start(
+                out=xs_plane[4 + r : P : 32, :].bitcast(I32), in_=xs_scales[0, r:16:4, :].bitcast(I32)
+            )
+        load_plane(wo_plane, wo_scales, nc.gpsimd)
         wa_raw[0, 0] = load_weight("wa00", wa, 0, 0, halves=1)
         load_tab(1, 1)
         wa_raw[1, 0] = load_weight("wa10", wa, 1, 0, halves=1)
@@ -119,17 +130,13 @@ def tile_list_larval_feeding_scores_kernel(
         wa_raw[1, 1] = load_weight("wa11", wa, 1, 1, halves=1)
         wd_raw[0, 0] = load_weight("wd00", wd, 0, 0, halves=1)
         nc.sync.dma_start(out=xs_codes[:].bitcast(I32), in_=xs_words[0].rearrange("p n t -> p (n t)").bitcast(I32))
-        for r in range(4):
-            nc.sync.dma_start(
-                out=xs_plane[4 + r : P : 32, :].bitcast(I32), in_=xs_scales[0, r:16:4, :].bitcast(I32)
-            )
         wd_raw[1, 0] = load_weight("wd10", wd, 1, 0, halves=1)
         wx_raw[0] = load_weight("wx0", wx, 0, 0, halves=1)
         wd_raw[0, 1] = load_weight("wd01", wd, 0, 1, halves=1)
-        load_plane(wo_plane, wo_scales)
-        nc.sync.dma_start(out=wo_codes[:].bitcast(I32), in_=wo_words.rearrange("g p c -> p g c").bitcast(I32))
+        nc.sync.dma_start(out=wo_codes[0][:].bitcast(I32), in_=wo_words[0].bitcast(I32))
         wd_raw[1, 1] = load_weight("wd11", wd, 1, 1, halves=1)
         wx_raw[1] = load_weight("wx1", wx, 0, 1, halves=2)
+        nc.sync.dma_start(out=wo_codes[1][:].bitcast(I32), in_=wo_words[1].bitcast(I32))
 
         wb_codes = sb("wb_codes", [P, 2, 2, PASS], U16)
         for b in range(2):
@@ -213,14 +220,16 @@ def tile_list_larval_feeding_scores_kernel(
                         stop=(last and t == PACK - 1),
                     )
 
-        def features(b, c, prod, bank):
+        def features(b, c, prod, bank, parts=1):
             h = sb(f"h{b}{c}", [P, CH, PACK], BF16)
-            nc.vector.tensor_tensor(
-                out=h[:].rearrange("p (q i) t -> p q t i", i=2),
-                in0=prod[:, :, c * CH : (c + 1) * CH].rearrange("p t (q i) -> p q t i", i=2),
-                in1=bank[:].rearrange("p (t q i) -> p q t i", t=PACK, i=2),
-                op=ALU.subtract,
-            )
+            step = CH // 2 // parts
+            for q0 in range(0, CH // 2, step):
+                nc.vector.tensor_tensor(
+                    out=h[:].rearrange("p (q i) t -> p q t i", i=2)[:, q0 : q0 + step],
+                    in0=prod[:, :, c * CH : (c + 1) * CH].rearrange("p t (q i) -> p q t i", i=2)[:, q0 : q0 + step],
+                    in1=bank[:].rearrange("p (t q i) -> p q t i", t=PACK, i=2)[:, q0 : q0 + step],
+                    op=ALU.subtract,
+                )
             return h
 
         def quantise_h(b, c, h):
@@ -233,7 +242,7 @@ def tile_list_larval_feeding_scores_kernel(
             rows = slice(nt * P, (nt + 1) * P)
             nc.tensor.matmul_mx(
                 out=dst,
-                lhsT=wo_codes[:, g, rows].bitcast(FP4X4),
+                lhsT=wo_codes[g][:, rows].bitcast(FP4X4),
                 lhsT_scale=wo_plane[:, g, rows],
                 rhs=hq[0][:].bitcast(FP8X4),
                 rhs_scale=hq[1][:],
@@ -277,20 +286,20 @@ def tile_list_larval_feeding_scores_kernel(
         wq["wd01"] = quantise_weight("wd01", wd_raw[0, 1], 1.0)
         product_d(ebank, wq["wd01"], v_codes[0], lambda cols: v_scales(0, cols), True, False)
         wq["wd11"] = quantise_weight("wd11", wd_raw[1, 1], 1.0)
+        wq["wx1"] = quantise_weight("wx1", wx_raw[1], -1.0, halves=2)
         product_d(ebank, wq["wd11"], v_codes[1], lambda cols: v_scales(1, cols), False, False)
+        product_d(ebank, wq["wx1"], xs_codes, xs_scales_at, False, True)
         h0 = [features(0, c, prod[0], xbank[c]) for c in range(NCH)]
         hq0 = [quantise_h(0, c, h0[c]) for c in range(NCH)]
         for c in range(NCH):
             for nt in range(NT - 1):
                 score_pass(xbank[c][:, nt * CH : (nt + 1) * CH], 0, nt, hq0[c], nt == 0, False)
-        wq["wx1"] = quantise_weight("wx1", wx_raw[1], -1.0, halves=2)
-        product_d(ebank, wq["wx1"], xs_codes, xs_scales_at, False, True)
 
         out_rows = out.rearrange("(nt p) j -> p nt j", p=P)
         h1 = [features(1, 0, prod[1], ebank[0])]
         for c in range(NCH):
             if c + 1 < NCH:
-                h1.append(features(1, c + 1, prod[1], ebank[c + 1]))
+                h1.append(features(1, c + 1, prod[1], ebank[c + 1], parts=2))
             hq1 = quantise_h(1, c, h1[c])
             score_pass(ebank[c][:, 0:CH], 0, NT - 1, hq0[c], True, False)
             for nt in range(NT - 1):

from contextlib import ExitStack

import concourse.mybir as mybir

K, T, S, K2, H, N = 1024, 2048, 512, 512, 1024, 640
FLOPS = 2 * S * (3 * K * H + K2 * H + H * N)

F32 = mybir.dt.float32
BF16 = mybir.dt.bfloat16
I32 = mybir.dt.int32
U32 = mybir.dt.uint32
U16 = mybir.dt.uint16
U8 = mybir.dt.uint8
FP8X4 = mybir.dt.float8_e4m3fn_x4
FP4X4 = mybir.dt.float4_e2m1fn_x4
ACT = mybir.ActivationFunctionType
ALU = mybir.AluOpType

P = 128
PACK = 4
PASS = P * PACK
CH = 128
NCH = S // CH
NT = N // P
SCALAR_M = 96
SCALAR_M_LAST = 24
SHARE = {"wa00":128,"wa10":64,"wa01":40,"wa11":40,"wd00":64,"wd10":32,"wx0":48,"wd01":80,"wd11":80,"wx1":24}


def tile_list_larval_feeding_scores_kernel(
    tc, tab_words, tab_scales, offs, xs_words, xs_scales, wa, ba, wb_words, wb_scales, wd, wx, wo_words, wo_scales, out
):
    nc = tc.nc
    with ExitStack() as ctx:
        keep = ctx.enter_context(tc.tile_pool(name="keep", bufs=1))
        ring = ctx.enter_context(tc.tile_pool(name="ring", bufs=4))
        psum = ctx.enter_context(tc.psum_pool(name="psum", bufs=1))

        def sb(name, shape, dtype):
            return keep.tile(shape, dtype, name=name, align_bytes=64)

        offsets = sb("offsets", [P, S // 16], U16)
        xbank = [psum.tile([P, PASS], F32, name=f"xbank{i}") for i in range(4)]
        ebank = [psum.tile([P, PASS], F32, name=f"ebank{i}") for i in range(4)]

        tab_plane = sb("tab_plane", [P, 2, T], U8)
        wb_plane_raw = sb("wb_plane_raw", [P, 2, H], U8)
        xs_plane = sb("xs_plane", [P, S], U8)
        wo_plane = sb("wo_plane", [P, 2, N], U8)
        nc.vector.memset(tab_plane[:, 0, :].bitcast(I32), 0)
        nc.gpsimd.memset(tab_plane[:, 1, :].bitcast(I32), 0)
        nc.vector.memset(wb_plane_raw[:].bitcast(I32), 0)
        for plane in (xs_plane, wo_plane):
            nc.gpsimd.memset(plane[:].bitcast(I32), 0)

        def load_weight(name, w, g, b, halves=1):
            raw = sb(name + "_raw", [P, PACK, PASS], F32)
            rows = w[g * PASS : (g + 1) * PASS, b * PASS : (b + 1) * PASS].rearrange("(p j) c -> p j c", j=PACK)
            if halves == PACK:
                for j in range(PACK):
                    nc.sync.dma_start(out=raw[:, j, :], in_=rows[:, j, :])
                return raw
            step = PASS // halves
            for c0 in range(0, PASS, step):
                nc.sync.dma_start(out=raw[:, :, c0 : c0 + step], in_=rows[:, :, c0 : c0 + step])
            return raw

        def quantise_weight(name, raw, sign, halves=1):
            scalar_m = SHARE[name]
            grouped = ring.tile([P, PACK, P, PACK], BF16, name="grouped", align_bytes=64)
            codes = sb(name + "_codes", [P, PASS], U32)
            plane = sb(name + "_plane", [P, PASS], U8)
            src = raw[:].rearrange("p j (m u i) -> p u m j i", u=2, i=2)
            dst = grouped[:].rearrange("p (u i) m j -> p u m j i", i=2)
            step = P // halves
            for m0 in range(0, P, step):
                m1 = m0 + step
                mid = m1 if m1 < P and halves > 1 else m0 + scalar_m
                for u in range(2):
                    if mid > m0:
                        nc.scalar.activation(out=dst[:, u, m0:mid], in_=src[:, u, m0:mid], func=ACT.Copy, scale=sign)
                    if m1 > mid:
                        nc.vector.tensor_scalar(
                            out=dst[:, u, mid:m1], in0=src[:, u, mid:m1], scalar1=sign, scalar2=None, op0=ALU.mult
                        )
            for u in range(halves):
                ts_ = slice(u * PACK // halves, (u + 1) * PACK // halves)
                cols = slice(ts_.start * P, ts_.stop * P)
                nc.vector.quantize_mx(
                    out=codes[:, cols].bitcast(FP8X4),
                    scales=plane[:, cols],
                    in_=grouped[:, ts_].rearrange("p t m j -> p (t m j)"),
                )
            return codes, plane

        wb_raw = sb("wb_raw", [P, 2, H], U16)
        bias = sb("bias", [P, 2, PACK], F32)
        tab = [sb(f"tab{g}", [P, T], U32) for g in range(2)]
        xs_codes = sb("xs_codes", [P, S], U32)
        wo_codes = [sb(f"wo_codes{g}", [P, N], U16) for g in range(2)]
        wa_raw, wd_raw, wx_raw = {}, {}, {}

        def load_plane(plane, scales, eng=nc.sync):
            for r in range(4):
                eng.dma_start(
                    out=plane[r:P:32].bitcast(I32),
                    in_=scales[:, r:16:4, :].rearrange("g q n -> q g n").bitcast(I32),
                )

        def load_tab(g, parts):
            words = tab_words[g].rearrange("p n t -> p (n t)").bitcast(I32)
            for c0 in range(0, T, T // parts):
                nc.sync.dma_start(out=tab[g][:, c0 : c0 + T // parts].bitcast(I32), in_=words[:, c0 : c0 + T // parts])

        nc.sync.dma_start(offsets[:], offs)
        nc.sync.dma_start(out=bias[:], in_=ba.rearrange("(b p t) -> p b t", b=2, t=PACK))
        nc.sync.dma_start(out=wb_raw[:].bitcast(I32), in_=wb_words.rearrange("g p c -> p g c").bitcast(I32))
        load_plane(tab_plane, tab_scales)
        load_tab(0, 1)
        load_plane(wb_plane_raw, wb_scales)
        for r in range(4):
            nc.gpsimd.dma_start(
                out=xs_plane[4 + r : P : 32, :].bitcast(I32), in_=xs_scales[0, r:16:4, :].bitcast(I32)
            )
        load_plane(wo_plane, wo_scales, nc.gpsimd)
        wa_raw[0, 0] = load_weight("wa00", wa, 0, 0, halves=1)
        load_tab(1, 1)
        wa_raw[1, 0] = load_weight("wa10", wa, 1, 0, halves=1)
        wa_raw[0, 1] = load_weight("wa01", wa, 0, 1, halves=1)
        wa_raw[1, 1] = load_weight("wa11", wa, 1, 1, halves=1)
        wd_raw[0, 0] = load_weight("wd00", wd, 0, 0, halves=1)
        nc.sync.dma_start(out=xs_codes[:].bitcast(I32), in_=xs_words[0].rearrange("p n t -> p (n t)").bitcast(I32))
        wd_raw[1, 0] = load_weight("wd10", wd, 1, 0, halves=1)
        wx_raw[0] = load_weight("wx0", wx, 0, 0, halves=1)
        wd_raw[0, 1] = load_weight("wd01", wd, 0, 1, halves=1)
        nc.sync.dma_start(out=wo_codes[0][:].bitcast(I32), in_=wo_words[0].bitcast(I32))
        wd_raw[1, 1] = load_weight("wd11", wd, 1, 1, halves=1)
        wx_raw[1] = load_weight("wx1", wx, 0, 1, halves=2)
        nc.sync.dma_start(out=wo_codes[1][:].bitcast(I32), in_=wo_words[1].bitcast(I32))

        wb_codes = sb("wb_codes", [P, 2, 2, PASS], U16)
        for b in range(2):
            for g in range(2):
                nc.scalar.copy(
                    out=wb_codes[:, g, b, :].rearrange("p (t u i) -> p u t i", t=PACK, i=8),
                    in_=wb_raw[:, g, b * PASS : (b + 1) * PASS].rearrange("p (u i t) -> p u t i", t=PACK, i=8),
                )

        v_plane = [sb(f"v_plane{g}", [P, S], U8) for g in range(2)]
        v_codes = [sb(f"v_codes{g}", [P, S], U32) for g in range(2)]
        wb_plane = sb("wb_plane", [P, 2, 2, PASS], U8)

        def gather_words(g):
            nc.vector.tensor_copy(v_codes[g][:], tab[g][:].indirect(offsets[:]))

        def gather_scales(g):
            nc.vector.tensor_copy(v_plane[g][:], tab_plane[:, g, :].indirect(offsets[:]))

        def deal_wb_scales(b):
            nc.vector.tensor_copy(
                out=wb_plane[:, :, b, :].rearrange("p g (t u i) -> p g u t i", t=PACK, i=16),
                in_=wb_plane_raw[:, :, b * PASS : (b + 1) * PASS].rearrange("p g (u i t) -> p g u t i", t=PACK, i=16),
            )

        def v_scales(g, cols):
            return v_plane[g][:, cols]

        def product_b(b, g, banks):
            for t in range(PACK):
                tc_ = slice(t * P, (t + 1) * P)
                nc.tensor.matmul_mx(
                    out=banks[t][:],
                    lhsT=wb_codes[:, g, b, tc_].bitcast(FP4X4),
                    lhsT_scale=wb_plane[:, g, b, tc_],
                    rhs=v_codes[g][:].bitcast(FP8X4),
                    rhs_scale=v_plane[g][:],
                    start=(g == 0),
                    stop=(g == 1),
                )

        def product_a(b, g):
            codes, plane = wq[f"wa{g}{b}"]
            for t in range(PACK):
                tc_ = slice(t * P, (t + 1) * P)
                nc.tensor.matmul_mx(
                    out=xbank[t][:],
                    lhsT=codes[:, tc_].bitcast(FP8X4),
                    lhsT_scale=plane[:, tc_],
                    rhs=v_codes[g][:].bitcast(FP8X4),
                    rhs_scale=v_scales(g, slice(0, S)),
                    start=(g == 0),
                    stop=(g == 1),
                )

        def squash(b):
            tanh_a = sb(f"tanh{b}", [P, PACK, S], F32)
            for t in range(PACK):
                nc.scalar.activation(out=tanh_a[:, t, :], in_=xbank[t][:], func=ACT.Tanh, bias=bias[:, b, t : t + 1])
            return tanh_a

        def gate(b, tanh_a, banks):
            prod = sb(f"prod{b}", [P, PACK, S], F32)
            for t in range(PACK):
                nc.vector.tensor_tensor(out=prod[:, t, :], in0=banks[t][:], in1=tanh_a[:, t, :], op=ALU.mult)
            return prod

        def product_d(banks, weights, moving, moving_plane, first, last, chunks=range(NCH)):
            codes, plane = weights
            for c in chunks:
                cols = slice(c * CH, (c + 1) * CH)
                for t in range(PACK):
                    tc_ = slice(t * P, (t + 1) * P)
                    nc.tensor.matmul_mx(
                        out=banks[c][:, tc_],
                        lhsT=codes[:, tc_].bitcast(FP8X4),
                        lhsT_scale=plane[:, tc_],
                        rhs=moving[:, cols].bitcast(FP8X4),
                        rhs_scale=moving_plane(cols),
                        start=(first and t == 0),
                        stop=(last and t == PACK - 1),
                    )

        def features(b, c, prod, bank, parts=1):
            h = sb(f"h{b}{c}", [P, CH, PACK], BF16)
            step = CH // 2 // parts
            for q0 in range(0, CH // 2, step):
                nc.vector.tensor_tensor(
                    out=h[:].rearrange("p (q i) t -> p q t i", i=2)[:, q0 : q0 + step],
                    in0=prod[:, :, c * CH : (c + 1) * CH].rearrange("p t (q i) -> p q t i", i=2)[:, q0 : q0 + step],
                    in1=bank[:].rearrange("p (t q i) -> p q t i", t=PACK, i=2)[:, q0 : q0 + step],
                    op=ALU.subtract,
                )
            return h

        def quantise_h(b, c, h):
            codes = sb(f"h{b}{c}_codes", [P, CH], U32)
            plane = sb(f"h{b}{c}_plane", [P, CH], U8)
            nc.vector.quantize_mx(out=codes[:].bitcast(FP8X4), scales=plane[:], in_=h[:].rearrange("p j t -> p (j t)"))
            return codes, plane

        def score_pass(dst, g, nt, hq, start, stop):
            rows = slice(nt * P, (nt + 1) * P)
            nc.tensor.matmul_mx(
                out=dst,
                lhsT=wo_codes[g][:, rows].bitcast(FP4X4),
                lhsT_scale=wo_plane[:, g, rows],
                rhs=hq[0][:].bitcast(FP8X4),
                rhs_scale=hq[1][:],
                start=start,
                stop=stop,
            )

        def xs_scales_at(cols):
            return xs_plane[4:, cols]

        wq, tanh_a, prod = {}, {}, {}
        gather_scales(0)
        gather_scales(1)
        gather_words(0)
        deal_wb_scales(0)
        gather_words(1)
        wq["wa00"] = quantise_weight("wa00", wa_raw[0, 0], 1.0)
        deal_wb_scales(1)
        wq["wa10"] = quantise_weight("wa10", wa_raw[1, 0], 1.0)
        product_a(0, 0)
        product_a(0, 1)
        product_b(0, 0, ebank)
        product_b(0, 1, ebank)
        tanh_a[0] = squash(0)
        wq["wa01"] = quantise_weight("wa01", wa_raw[0, 1], 1.0)
        product_a(1, 0)
        wq["wa11"] = quantise_weight("wa11", wa_raw[1, 1], 1.0)
        product_a(1, 1)
        tanh_a[1] = squash(1)
        prod[0] = gate(0, tanh_a[0], ebank)
        product_b(1, 0, ebank)
        product_b(1, 1, ebank)
        wq["wd00"] = quantise_weight("wd00", wd_raw[0, 0], 1.0)
        wq["wd10"] = quantise_weight("wd10", wd_raw[1, 0], 1.0)
        wq["wx0"] = quantise_weight("wx0", wx_raw[0], -1.0)
        prod[1] = gate(1, tanh_a[1], ebank)
        product_d(xbank, wq["wd00"], v_codes[0], lambda cols: v_scales(0, cols), True, False)
        for c in range(NCH):
            product_d(xbank, wq["wd10"], v_codes[1], lambda cols: v_scales(1, cols), False, False, [c])
            product_d(xbank, wq["wx0"], xs_codes, xs_scales_at, False, True, [c])
        wq["wd01"] = quantise_weight("wd01", wd_raw[0, 1], 1.0)
        product_d(ebank, wq["wd01"], v_codes[0], lambda cols: v_scales(0, cols), True, False)
        wq["wd11"] = quantise_weight("wd11", wd_raw[1, 1], 1.0)
        wq["wx1"] = quantise_weight("wx1", wx_raw[1], -1.0, halves=2)
        product_d(ebank, wq["wd11"], v_codes[1], lambda cols: v_scales(1, cols), False, False)
        product_d(ebank, wq["wx1"], xs_codes, xs_scales_at, False, True)
        h0 = [features(0, c, prod[0], xbank[c]) for c in range(NCH)]
        hq0 = [quantise_h(0, c, h0[c]) for c in range(NCH)]
        for c in range(NCH):
            for nt in range(NT - 1):
                score_pass(xbank[c][:, nt * CH : (nt + 1) * CH], 0, nt, hq0[c], nt == 0, False)

        out_rows = out.rearrange("(nt p) j -> p nt j", p=P)
        h1 = [features(1, 0, prod[1], ebank[0])]
        for c in range(NCH):
            if c + 1 < NCH:
                h1.append(features(1, c + 1, prod[1], ebank[c + 1], parts=2))
            hq1 = quantise_h(1, c, h1[c])
            score_pass(ebank[c][:, 0:CH], 0, NT - 1, hq0[c], True, False)
            for nt in range(NT - 1):
                score_pass(xbank[c][:, nt * CH : (nt + 1) * CH], 1, nt, hq1, False, nt == NT - 2)
            score_pass(ebank[c][:, 0:CH], 1, NT - 1, hq1, False, True)
            scores = sb(f"scores{c}", [P, NT, CH], F32)
            nc.scalar.copy(out=scores[:, 0 : NT - 1, :].rearrange("p n j -> p (n j)"), in_=xbank[c][:])
            if c + 1 < NCH:
                nc.scalar.copy(out=scores[:, NT - 1, :], in_=ebank[c][:, 0:CH])
            else:
                nc.vector.tensor_copy(out=scores[:, NT - 1, :], in_=ebank[c][:, 0:CH])
            nc.sync.dma_start(out=out_rows[:, :, c * CH : (c + 1) * CH], in_=scores[:])
